import numpy as np
import ml_dtypes


def mxq(x, axis, fmt="e4m3"):
    dtype, down = {"e4m3": (ml_dtypes.float8_e4m3fn, 7), "e5m2": (ml_dtypes.float8_e5m2, 14)}[fmt]
    v = np.moveaxis(np.asarray(x, np.float32).astype(ml_dtypes.bfloat16).astype(np.float64), axis, -1)
    blocks = v.reshape(v.shape[:-1] + (-1, 32))
    amax = np.abs(blocks).max(-1, keepdims=True)
    byte = np.maximum(np.where(amax > 0, np.frexp(amax)[1] - 1 + 127, 0) - down, 1)
    scale = np.exp2(byte - 127.0)
    codes = (blocks / scale).astype(np.float32).astype(dtype).astype(np.float64)
    return np.moveaxis((codes * scale).reshape(v.shape), -1, axis)


WIDE = False


def mx_kscale(k):
    if not WIDE:
        return np.ones(k)
    levels = np.array([10, -10, 5, -5, 0])
    if k % 512:
        return np.exp2(np.random.permutation(np.resize(levels, k // 32))).repeat(32)
    a = np.empty((k // 512, 16))
    for p in range(k // 512):
        a[p, :8] = np.random.permutation(np.resize(levels, 8))
        for g in range(8):
            far = levels[np.abs(levels - a[p, g]) >= 10]
            a[p, g + 8] = far[np.random.randint(len(far))]
    return np.exp2(a.ravel()).repeat(32)


def f64(x):
    return np.asarray(x).astype(np.float64)


def striped(idx):
    return np.tile(np.asarray(idx).reshape(-1, 16).T, (8, 1)).astype(np.uint16)


def unstriped(offs):
    return offs[:16].T.reshape(-1).astype(np.int64)


def striped8(idx):
    return np.asarray(idx).reshape(8, -1, 16).transpose(0, 2, 1).reshape(128, -1).astype(np.uint16)


def unstriped8(offs):
    return offs.reshape(8, 16, -1).transpose(0, 2, 1).reshape(8, -1).astype(np.int64)


def pick8(x, idx, run):
    r = np.arange(len(x))
    return x[r[:, None], idx[r % (8 * run) // run]]


E2M1 = np.array([0.0, 0.5, 1.0, 1.5, 2.0, 3.0, 4.0, 6.0, -0.0, -0.5, -1.0, -1.5, -2.0, -3.0, -4.0, -6.0])


def pack_weight(w, fmt):
    k, n = w.shape
    w = f64(np.asarray(w, np.float32).astype(ml_dtypes.bfloat16)).reshape(k // 32, 32, n)
    amax = np.abs(w).max(1)
    if fmt == "e4m3":
        byte = np.frexp(amax)[1] - 1 + 127 - 7
    else:
        mant, ex = np.frexp(amax / 6.0)
        byte = np.where(mant > 0.5, ex, ex - 1) + 127
    byte = np.clip(np.where(amax > 0, byte, 1), 1, 254)
    scaled = (w * np.exp2(127.0 - byte)[:, None, :]).reshape(k, n).astype(np.float32)
    by_word = np.ascontiguousarray(scaled.reshape(k // 512, 128, 4, n).transpose(0, 1, 3, 2))
    if fmt == "e4m3":
        words = by_word.astype(ml_dtypes.float8_e4m3fn).view(np.uint8)
    else:
        c = by_word.astype(ml_dtypes.float4_e2m1fn).view(np.uint8) & 0xF
        words = (c[..., 0::2] | (c[..., 1::2] << 4)).reshape(k // 512, 128, 2 * n)
    return np.ascontiguousarray(words), np.ascontiguousarray(byte.astype(np.uint8).reshape(k // 512, 16, n))


def unpack_weight(words, scales, fmt):
    g, _, n = scales.shape
    words = np.ascontiguousarray(words).reshape(g, 128, n, -1)
    if fmt == "e4m3":
        vals = words.view(ml_dtypes.float8_e4m3fn).astype(np.float64)
    else:
        nib = np.empty((g, 128, n, 4), np.uint8)
        nib[..., 0::2] = words & 0xF
        nib[..., 1::2] = words >> 4
        vals = E2M1[nib]
    vals = vals * np.repeat(np.exp2(scales.astype(np.float64) - 127.0), 8, axis=1)[..., None]
    return vals.transpose(0, 1, 3, 2).reshape(g * 512, n)


K, J, R, T, Z, M, O, C, N, S = 512, 512, 512, 1024, 512, 1024, 192, 256, 256, 1024


def setup_inputs():
    n = np.random.standard_normal
    idx = np.random.permutation(T)[:J]
    idx2 = np.random.permutation(M)[:J]
    idx3 = np.stack([np.random.permutation(J)[:O] for _ in range(8)])
    idx4 = np.stack([np.random.permutation(C)[:O] for _ in range(8)])
    idx5 = np.stack([np.random.permutation(J)[:C] for _ in range(8)])
    idx6 = np.random.permutation(S)[:N]
    fk = mx_kscale(K)
    fr = mx_kscale(R)
    fz = mx_kscale(Z)
    xtp = pack_weight(n((K, T)) * fk[:, None], "e2m1")
    wp = pack_weight(n((K, R)) * 1 / np.sqrt(K) / fk[:, None] * fr, "e4m3")
    xop = pack_weight(n((Z, M)) / fz[:, None], "e2m1")
    w2p = pack_weight(n((Z, R)) * 1 / np.sqrt(Z) * fz[:, None] * fr, "e4m3")
    vsp = pack_weight(n((R, S)) * 1 / np.sqrt(R) / fr[:, None], "e4m3")
    return {
        "xt_words": xtp[0],
        "xt_scales": xtp[1],
        "w_words": wp[0],
        "w_scales": wp[1],
        "xo_words": xop[0],
        "xo_scales": xop[1],
        "w2_words": w2p[0],
        "w2_scales": w2p[1],
        "sa": (np.random.uniform(0.5, 1.6, (R, 1))).astype(np.float32),
        "sb": (np.random.uniform(0.5, 1.6, (R, 1))).astype(np.float32),
        "vs_words": vsp[0],
        "vs_scales": vsp[1],
        "offs": striped(idx),
        "offs2": striped(idx2),
        "offs3": striped8(idx3),
        "offs4": striped8(idx4),
        "offs5": striped8(idx5),
        "offs6": striped(idx6),
    }


def reference(xt_words, xt_scales, w_words, w_scales, xo_words, xo_scales, w2_words, w2_scales, sa, sb, vs_words, vs_scales, offs, offs2, offs3, offs4, offs5, offs6):
    idx = unstriped(offs)
    idx2 = unstriped(offs2)
    idx3 = unstriped8(offs3)
    idx4 = unstriped8(offs4)
    idx5 = unstriped8(offs5)
    idx6 = unstriped(offs6)
    xtu = unpack_weight(xt_words, xt_scales, "e2m1")
    wu = unpack_weight(w_words, w_scales, "e4m3")
    xou = unpack_weight(xo_words, xo_scales, "e2m1")
    w2u = unpack_weight(w2_words, w2_scales, "e4m3")
    vsu = unpack_weight(vs_words, vs_scales, "e4m3")
    xtidxg = xtu[:, idx]
    a = wu.T @ xtidxg
    xoidx2g = xou[:, idx2]
    b = w2u.T @ xoidx2g
    h1 = pick8(a, idx3, 64) * f64(sa)
    pw = np.zeros((R, C))
    pw[np.arange(R)[:, None], idx4[np.arange(R) % 512 // 64]] = h1
    hid = np.maximum(pw, pick8(b, idx5, 64) * f64(sb))
    vsidx6g = vsu[:, idx6]
    hidq = mxq(hid, 0, "e4m3")
    y = vsidx6g.T @ hidq
    return y

@@ -1,0 +1,179 @@
+from contextlib import ExitStack
+
+import concourse.mybir as mybir
+
+F32 = mybir.dt.float32
+BF16 = mybir.dt.bfloat16
+I32 = mybir.dt.int32
+U32 = mybir.dt.uint32
+U16 = mybir.dt.uint16
+U8 = mybir.dt.uint8
+FP8X4 = mybir.dt.float8_e4m3fn_x4
+FP4X4 = mybir.dt.float4_e2m1fn_x4
+COPY = mybir.ActivationFunctionType.Copy
+MAX = mybir.AluOpType.max
+
+P = 128
+PACK = 4
+J, R, T, O, C, N, S = 512, 512, 1024, 192, 256, 256, 1024
+FLOPS = 2 * 512 * R * J * 2 + 2 * R * N * C
+
+
+def tile_picked_tokens_plain_two_filledpage_store_plain_kernel(
+    tc, xt_words, xt_scales, w_words, w_scales, xo_words, xo_scales, w2_words, w2_scales, sa, sb,
+    vs_words, vs_scales, offs, offs2, offs3, offs4, offs5, offs6, out,
+):
+    nc = tc.nc
+    with ExitStack() as ctx:
+        keep = ctx.enter_context(tc.tile_pool(name="keep", bufs=1))
+        psum = ctx.enter_context(tc.psum_pool(name="psum", bufs=8))
+
+        def sb_tile(name, shape, dtype):
+            return keep.tile(shape, dtype, name=name, align_bytes=64)
+
+        def load_list(name, src):
+            tile = sb_tile(name, [P, src.shape[1]], U16)
+            nc.sync.dma_start(tile[:], src)
+            return tile
+
+        def zeroed_plane(name, width):
+            tile = sb_tile(name, [P, width], U8)
+            nc.vector.memset(tile[:].bitcast(I32), 0)
+            return tile
+
+        def load_plane(queue, tile, src):
+            for q in range(4):
+                queue.dma_start(tile[32 * q : 32 * q + 4, :].bitcast(I32), src[0, 4 * q : 4 * q + 4, :].bitcast(I32))
+
+        def load_fp4(name, src):
+            tile = sb_tile(name, [P, T], U16)
+            nc.sync.dma_start(tile[:].bitcast(I32), src[0].bitcast(I32))
+            return tile
+
+        def load_fp8(name, src):
+            tile = sb_tile(name, [P, src.shape[2]], U32)
+            nc.sync.dma_start(tile[:].bitcast(I32), src[0].rearrange("p n t -> p (n t)").bitcast(I32))
+            return tile
+
+        def load_gain(name, src):
+            tile = sb_tile(name, [P, PACK], F32)
+            nc.gpsimd.dma_start(tile[:], src.rearrange("(p t) o -> p (t o)", t=PACK))
+            return tile
+
+        xt_plane = zeroed_plane("xt_plane", T)
+        w_plane = zeroed_plane("w_plane", R)
+        xo_plane = zeroed_plane("xo_plane", T)
+        w2_plane = zeroed_plane("w2_plane", R)
+        vs_plane = zeroed_plane("vs_plane", S)
+        pages = [sb_tile(f"page{t}", [P, C], F32) for t in range(PACK)]
+        for page in pages:
+            nc.vector.memset(page[:], 0.0)
+
+        load_plane(nc.scalar, xt_plane, xt_scales)
+        l1 = load_list("l1", offs)
+        xt_sb = load_fp4("xt_sb", xt_words)
+        w_sb = load_fp8("w_sb", w_words)
+        load_plane(nc.sync, w_plane, w_scales)
+        sa_sb = load_gain("sa_sb", sa)
+        sb_sb = load_gain("sb_sb", sb)
+        l2 = load_list("l2", offs2)
+        xo_sb = load_fp4("xo_sb", xo_words)
+        l3 = load_list("l3", offs3)
+        l4 = load_list("l4", offs4)
+        load_plane(nc.sync, xo_plane, xo_scales)
+        w2_sb = load_fp8("w2_sb", w2_words)
+        load_plane(nc.sync, w2_plane, w2_scales)
+        l5 = load_list("l5", offs5)
+        l6 = load_list("l6", offs6)
+        vs_sb = load_fp8("vs_sb", vs_words)
+        load_plane(nc.sync, vs_plane, vs_scales)
+
+        def deal(name, words, plane):
+            dealt_words = sb_tile(name + "_words", [P, R], U32)
+            dealt_plane = sb_tile(name + "_plane", [P, R], U8)
+            nc.scalar.copy(
+                dealt_words[:].rearrange("p (t m) -> p m t", t=PACK), words[:].rearrange("p (m t) -> p m t", t=PACK)
+            )
+            nc.vector.tensor_copy(
+                dealt_plane[:].rearrange("p (t m) -> p m t", t=PACK), plane[:].rearrange("p (m t) -> p m t", t=PACK)
+            )
+            return dealt_words, dealt_plane
+
+        def pick(name, words, plane, offsets, count, dtype):
+            picked_words = sb_tile(name + "_words", [P, count], dtype)
+            picked_plane = sb_tile(name + "_plane", [P, count], U8)
+            nc.vector.tensor_copy(picked_plane[:], plane[:].indirect(offsets[:]))
+            nc.vector.tensor_copy(picked_words[:], words[:].indirect(offsets[:]))
+            return picked_words, picked_plane
+
+        def product(name, t, dealt, picked, evacuate):
+            bank = psum.tile([P, J], F32, name="bank")
+            cols = slice(t * P, (t + 1) * P)
+            nc.tensor.matmul_mx(
+                out=bank[:], lhsT=dealt[0][:, cols].bitcast(FP8X4), lhsT_scale=dealt[1][:, cols],
+                rhs=picked[0][:].bitcast(FP4X4), rhs_scale=picked[1][:], start=True, stop=True,
+            )
+            rows = sb_tile(f"{name}{t}", [P, J], F32)
+            evacuate(rows[:], bank[:])
+            return rows
+
+        xt_picked = pick("xtp", xt_sb, xt_plane, l1, J, U16)
+        w_dealt = deal("wd", w_sb, w_plane)
+        w2_words_dealt = sb_tile("w2d_words", [P, R], U32)
+        nc.scalar.copy(
+            w2_words_dealt[:].rearrange("p (t m) -> p m t", t=PACK), w2_sb[:].rearrange("p (m t) -> p m t", t=PACK)
+        )
+
+        def fill(t, rows):
+            h1 = sb_tile(f"h1_{t}", [P, O], F32)
+            nc.scalar.activation(h1[:], rows[:].indirect(l3[:]), COPY, scale=sa_sb[:, t : t + 1])
+            nc.scalar.activation(pages[t][:].indirect(l4[:]), h1[:], COPY)
+
+        fill(0, product("a", 0, w_dealt, xt_picked, nc.scalar.copy))
+        xo_words_picked = sb_tile("xop_words", [P, J], U16)
+        xo_plane_picked = sb_tile("xop_plane", [P, J], U8)
+        nc.vector.tensor_copy(xo_words_picked[:], xo_sb[:].indirect(l2[:]))
+        fill(1, product("a", 1, w_dealt, xt_picked, nc.vector.tensor_copy))
+        nc.vector.tensor_copy(xo_plane_picked[:], xo_plane[:].indirect(l2[:]))
+        fill(2, product("a", 2, w_dealt, xt_picked, nc.vector.tensor_copy))
+        w2_plane_dealt = sb_tile("w2d_plane", [P, R], U8)
+        nc.vector.tensor_copy(
+            w2_plane_dealt[:].rearrange("p (t m) -> p m t", t=PACK), w2_plane[:].rearrange("p (m t) -> p m t", t=PACK)
+        )
+        fill(3, product("a", 3, w_dealt, xt_picked, nc.vector.tensor_copy))
+        b_rows = [
+            product("b", t, (w2_words_dealt, w2_plane_dealt), (xo_words_picked, xo_plane_picked), nc.vector.tensor_copy)
+            for t in range(PACK)
+        ]
+        vs_picked = pick("vsp", vs_sb, vs_plane, l6, N, U32)
+
+        half = C // 2
+        out_view = out.rearrange("(u p) c -> p u c", p=P)
+        for h in range(2):
+            cols = slice(h * half, (h + 1) * half)
+            fetched = sb_tile(f"fetched{h}", [P, PACK, half], F32)
+            hid = sb_tile(f"hid{h}", [P, PACK, half], BF16)
+            for t in range(PACK):
+                nc.scalar.activation(
+                    fetched[:, t, :], b_rows[t][:].indirect(l5[:, h * half // 16 : (h + 1) * half // 16]), COPY,
+                    scale=sb_sb[:, t : t + 1],
+                )
+                nc.vector.tensor_tensor(hid[:, t, :], pages[t][:, cols], fetched[:, t, :], MAX)
+            grouped = sb_tile(f"grouped{h}", [P, half, PACK], BF16)
+            nc.vector.tensor_copy(grouped[:], hid[:].rearrange("p t c -> p c t"))
+            codes = sb_tile(f"codes{h}", [P, half], U32)
+            scales = sb_tile(f"scales{h}", [P, half], U8)
+            nc.vector.quantize_mx(
+                out=codes[:].bitcast(FP8X4), scales=scales[:], in_=grouped[:].rearrange("p c t -> p (c t)")
+            )
+            bank = psum.tile([P, J], F32, name="bank")
+            for u in range(N // P):
+                nc.tensor.matmul_mx(
+                    out=bank[:, u * half : (u + 1) * half],
+                    lhsT=vs_picked[0][:, u * P : (u + 1) * P].bitcast(FP8X4),
+                    lhsT_scale=vs_picked[1][:, u * P : (u + 1) * P],
+                    rhs=codes[:].bitcast(FP8X4), rhs_scale=scales[:], start=True, stop=True,
+                )
+            result = sb_tile(f"result{h}", [P, N // P, half], F32)
+            nc.scalar.copy(result[:].rearrange("p u c -> p (u c)"), bank[:, 0 : N // P * half])
+            nc.sync.dma_start(out_view[:, :, cols], result[:])

@@ -26,132 +26,163 @@ def tile_picked_tokens_plain_two_filledpage_store_plain_kernel(
     nc = tc.nc
     with ExitStack() as ctx:
         keep = ctx.enter_context(tc.tile_pool(name="keep", bufs=1))
+        reused = ctx.enter_context(tc.tile_pool(name="reused", bufs=1))
         psum = ctx.enter_context(tc.psum_pool(name="psum", bufs=8))
 
         def sb_tile(name, shape, dtype):
             return keep.tile(shape, dtype, name=name, align_bytes=64)
+
+        def placed(name, shape, dtype, offset):
+            return reused.tile(shape, dtype, name=name, offset=offset, align_bytes=64)
+
+        def clock(name, src, dtype):
+            tile = sb_tile(name, [P, 1], dtype)
+            nc.gpsimd.tensor_copy(tile[:], src)
 
         def load_list(name, src):
             tile = sb_tile(name, [P, src.shape[1]], U16)
             nc.sync.dma_start(tile[:], src)
             return tile
 
-        def zeroed_plane(name, width):
-            tile = sb_tile(name, [P, width], U8)
-            nc.vector.memset(tile[:].bitcast(I32), 0)
+        def zero(engine, tile):
+            engine.memset(tile[:].bitcast(I32), 0)
             return tile
 
         def load_plane(queue, tile, src):
             for q in range(4):
                 queue.dma_start(tile[32 * q : 32 * q + 4, :].bitcast(I32), src[0, 4 * q : 4 * q + 4, :].bitcast(I32))
 
-        def load_fp4(name, src):
-            tile = sb_tile(name, [P, T], U16)
+        def load_folded_plane(queues, tile, src):
+            rows = src[0].bitcast(I32).rearrange("(a b i) n -> b i a n", a=2, b=2)
+            for b in range(2):
+                queues[b].dma_start(
+                    tile[32 * b : 32 * b + 4, :].bitcast(I32).rearrange("i (a n) -> i a n", a=2), rows[b]
+                )
+
+        def load_fp4(name, src, offset):
+            tile = placed(name, [P, T], U16, offset)
             nc.sync.dma_start(tile[:].bitcast(I32), src[0].bitcast(I32))
             return tile
 
-        def load_fp8(name, src):
+        def load_fp8(queue, name, src):
             tile = sb_tile(name, [P, src.shape[2]], U32)
-            nc.sync.dma_start(tile[:].bitcast(I32), src[0].rearrange("p n t -> p (n t)").bitcast(I32))
+            queue.dma_start(tile[:].bitcast(I32), src[0].rearrange("p n t -> p (n t)").bitcast(I32))
             return tile
 
         def load_gain(name, src):
             tile = sb_tile(name, [P, PACK], F32)
-            nc.gpsimd.dma_start(tile[:], src.rearrange("(p t) o -> p (t o)", t=PACK))
+            nc.sync.dma_start(tile[:], src.rearrange("(p t) o -> p (t o)", t=PACK))
             return tile
 
-        xt_plane = zeroed_plane("xt_plane", T)
-        w_plane = zeroed_plane("w_plane", R)
-        xo_plane = zeroed_plane("xo_plane", T)
-        w2_plane = zeroed_plane("w2_plane", R)
-        vs_plane = zeroed_plane("vs_plane", S)
+        xt_plane = zero(nc.vector, sb_tile("xt_plane", [P, T], U8))
+        w_folded = zero(nc.gpsimd, placed("w_folded", [P, 2 * R], U8, 512))
+        xo_plane = zero(nc.vector, placed("xo_plane", [P, T], U8, 11776))
+        w2_plane = zero(nc.vector, sb_tile("w2_plane", [P, R], U8))
+        vs_plane = zero(nc.vector, sb_tile("vs_plane", [P, S], U8))
+
         pages = [sb_tile(f"page{t}", [P, C], F32) for t in range(PACK)]
         for page in pages:
             nc.vector.memset(page[:], 0.0)
 
         load_plane(nc.scalar, xt_plane, xt_scales)
         l1 = load_list("l1", offs)
-        xt_sb = load_fp4("xt_sb", xt_words)
-        w_sb = load_fp8("w_sb", w_words)
-        load_plane(nc.sync, w_plane, w_scales)
-        sa_sb = load_gain("sa_sb", sa)
-        sb_sb = load_gain("sb_sb", sb)
-        l2 = load_list("l2", offs2)
-        xo_sb = load_fp4("xo_sb", xo_words)
+        xt_sb = load_fp4("xt_sb", xt_words, 5632)
+        w_sb = load_fp8(nc.gpsimd, "w_sb", w_words)
+        load_folded_plane((nc.sync, nc.sync), w_folded, w_scales)
+        load_plane(nc.gpsimd, w2_plane, w2_scales)
         l3 = load_list("l3", offs3)
+        sa_sb = load_gain("sa_sb", sa)
+        w2_sb = load_fp8(nc.sync, "w2_sb", w2_words)
         l4 = load_list("l4", offs4)
+        l2 = load_list("l2", offs2)
+        xo_sb = load_fp4("xo_sb", xo_words, 9728)
         load_plane(nc.sync, xo_plane, xo_scales)
-        w2_sb = load_fp8("w2_sb", w2_words)
-        load_plane(nc.sync, w2_plane, w2_scales)
-        l5 = load_list("l5", offs5)
         l6 = load_list("l6", offs6)
-        vs_sb = load_fp8("vs_sb", vs_words)
+        vs_sb = load_fp8(nc.sync, "vs_sb", vs_words)
         load_plane(nc.sync, vs_plane, vs_scales)
+        l5 = load_list("l5", offs5)
+        sb_sb = load_gain("sb_sb", sb)
 
-        def deal(name, words, plane):
-            dealt_words = sb_tile(name + "_words", [P, R], U32)
-            dealt_plane = sb_tile(name + "_plane", [P, R], U8)
-            nc.scalar.copy(
-                dealt_words[:].rearrange("p (t m) -> p m t", t=PACK), words[:].rearrange("p (m t) -> p m t", t=PACK)
-            )
-            nc.vector.tensor_copy(
-                dealt_plane[:].rearrange("p (t m) -> p m t", t=PACK), plane[:].rearrange("p (m t) -> p m t", t=PACK)
-            )
-            return dealt_words, dealt_plane
+        def deal(copy, dst, src):
+            copy(dst.rearrange("p (t m) -> p m t", t=PACK), src.rearrange("p (m t) -> p m t", t=PACK))
 
-        def pick(name, words, plane, offsets, count, dtype):
-            picked_words = sb_tile(name + "_words", [P, count], dtype)
-            picked_plane = sb_tile(name + "_plane", [P, count], U8)
-            nc.vector.tensor_copy(picked_plane[:], plane[:].indirect(offsets[:]))
-            nc.vector.tensor_copy(picked_words[:], words[:].indirect(offsets[:]))
-            return picked_words, picked_plane
+        def deal_plane(dealt, folded):
+            nc.vector.tensor_copy(folded[64:128, 0:R].bitcast(I32), folded[0:64, R : 2 * R].bitcast(I32))
+            deal(nc.vector.tensor_copy, dealt[:], folded[:, 0:R])
+            return dealt
 
-        def product(name, t, dealt, picked, evacuate):
+        def gather(dst, window, offsets):
+            nc.vector.tensor_copy(dst[:], window[:].indirect(offsets))
+            return dst
+
+        def product(t, dealt, picked):
+            width = picked[1].shape[1]
             bank = psum.tile([P, J], F32, name="bank")
             cols = slice(t * P, (t + 1) * P)
             nc.tensor.matmul_mx(
-                out=bank[:], lhsT=dealt[0][:, cols].bitcast(FP8X4), lhsT_scale=dealt[1][:, cols],
-                rhs=picked[0][:].bitcast(FP4X4), rhs_scale=picked[1][:], start=True, stop=True,
+                out=bank[:, 0:width], lhsT=dealt[0][:, cols].bitcast(FP8X4), lhsT_scale=dealt[1][:, cols],
+                rhs=picked[0].bitcast(FP4X4), rhs_scale=picked[1], start=True, stop=True,
             )
-            rows = sb_tile(f"{name}{t}", [P, J], F32)
-            evacuate(rows[:], bank[:])
-            return rows
+            return bank[:, 0:width]
 
-        xt_picked = pick("xtp", xt_sb, xt_plane, l1, J, U16)
-        w_dealt = deal("wd", w_sb, w_plane)
-        w2_words_dealt = sb_tile("w2d_words", [P, R], U32)
-        nc.scalar.copy(
-            w2_words_dealt[:].rearrange("p (t m) -> p m t", t=PACK), w2_sb[:].rearrange("p (m t) -> p m t", t=PACK)
+        a_rows = [sb_tile(f"a{t}", [P, J], F32) for t in range(PACK)]
+        b_rows = [sb_tile(f"b{t}", [P, J], F32) for t in range(PACK)]
+        hj = J // 2
+
+        w_words_dealt = placed("wd_words", [P, R], U32, 3072)
+        for t in (0, 2):
+            nc.scalar.copy(
+                w_words_dealt[:].rearrange("p (t m) -> p m t", t=PACK)[:, :, t : t + 2],
+                w_sb[:].rearrange("p (m t) -> p m t", t=PACK)[:, :, t : t + 2],
+            )
+        lo_words = gather(sb_tile("xt_lo_words", [P, hj], U16), xt_sb, l1[:, 0 : hj // 16])
+        lo_plane = gather(sb_tile("xt_lo_plane", [P, hj], U8), xt_plane, l1[:, 0 : hj // 16])
+        w_dealt = (w_words_dealt, deal_plane(placed("wd_plane", [P, R], U8, 2048), w_folded))
+        for t in range(PACK):
+            nc.scalar.copy(a_rows[t][:, 0:hj], product(t, w_dealt, (lo_words[:], lo_plane[:])))
+        hi_words = gather(
+            placed("xt_hi_words", [P, hj], U16, 512), xt_sb, l1[:, hj // 16 : J // 16]
         )
-
-        def fill(t, rows):
-            h1 = sb_tile(f"h1_{t}", [P, O], F32)
-            nc.scalar.activation(h1[:], rows[:].indirect(l3[:]), COPY, scale=sa_sb[:, t : t + 1])
-            nc.scalar.activation(pages[t][:].indirect(l4[:]), h1[:], COPY)
-
-        fill(0, product("a", 0, w_dealt, xt_picked, nc.scalar.copy))
-        xo_words_picked = sb_tile("xop_words", [P, J], U16)
-        xo_plane_picked = sb_tile("xop_plane", [P, J], U8)
-        nc.vector.tensor_copy(xo_words_picked[:], xo_sb[:].indirect(l2[:]))
-        fill(1, product("a", 1, w_dealt, xt_picked, nc.vector.tensor_copy))
-        nc.vector.tensor_copy(xo_plane_picked[:], xo_plane[:].indirect(l2[:]))
-        fill(2, product("a", 2, w_dealt, xt_picked, nc.vector.tensor_copy))
-        w2_plane_dealt = sb_tile("w2d_plane", [P, R], U8)
-        nc.vector.tensor_copy(
-            w2_plane_dealt[:].rearrange("p (t m) -> p m t", t=PACK), w2_plane[:].rearrange("p (m t) -> p m t", t=PACK)
+        hi_plane = gather(
+            placed("xt_hi_plane", [P, hj], U8, 1024), xt_plane, l1[:, hj // 16 : J // 16]
         )
-        fill(3, product("a", 3, w_dealt, xt_picked, nc.vector.tensor_copy))
-        b_rows = [
-            product("b", t, (w2_words_dealt, w2_plane_dealt), (xo_words_picked, xo_plane_picked), nc.vector.tensor_copy)
-            for t in range(PACK)
-        ]
-        vs_picked = pick("vsp", vs_sb, vs_plane, l6, N, U32)
+        for t in range(PACK):
+            evacuate = nc.scalar.copy if t == 0 else nc.vector.tensor_copy
+            evacuate(a_rows[t][:, hj:J], product(t, w_dealt, (hi_words[:], hi_plane[:])))
+
+        w2_words_dealt = placed("w2d_words", [P, R], U32, 5632)
+        deal(nc.vector.tensor_copy, w2_words_dealt[:], w2_sb[:])
+        h1 = [sb_tile(f"h1_{t}", [P, O], F32) for t in range(PACK)]
+
+        def fetch_a(t):
+            nc.scalar.activation(h1[t][:], a_rows[t][:].indirect(l3[:]), COPY, scale=sa_sb[:, t : t + 1])
+
+        def fill(t):
+            nc.scalar.activation(pages[t][:].indirect(l4[:]), h1[t][:], COPY)
+
+        for t in range(PACK):
+            fetch_a(t)
+        for t in range(PACK):
+            fill(t)
+
+
+        xo_picked = (
+            gather(placed("xop_words", [P, J], U16, 3072), xo_sb, l2[:])[:],
+            gather(placed("xop_plane", [P, J], U8, 4096), xo_plane, l2[:])[:],
+        )
+        w2_plane_dealt = placed("w2d_plane", [P, R], U8, 11776)
+        deal(nc.vector.tensor_copy, w2_plane_dealt[:], w2_plane[:])
+        w2_dealt = (w2_words_dealt, w2_plane_dealt)
+        vs_words_picked = gather(placed("vsp_words", [P, N], U32, 9728), vs_sb, l6[:])
+        for t in range(PACK):
+            nc.vector.tensor_copy(b_rows[t][:], product(t, w2_dealt, xo_picked))
+        vs_picked = (vs_words_picked, gather(placed("vsp_plane", [P, N], U8, 11776), vs_plane, l6[:]))
+        fetched_all = placed("fetched", [P, 2, PACK, C // 2], F32, 5632)
 
         half = C // 2
-        out_view = out.rearrange("(u p) c -> p u c", p=P)
         for h in range(2):
             cols = slice(h * half, (h + 1) * half)
-            fetched = sb_tile(f"fetched{h}", [P, PACK, half], F32)
+            fetched = fetched_all[:, h]
             hid = sb_tile(f"hid{h}", [P, PACK, half], BF16)
             for t in range(PACK):
                 nc.scalar.activation(
@@ -166,14 +197,16 @@ def tile_picked_tokens_plain_two_filledpage_store_plain_kernel(
             nc.vector.quantize_mx(
                 out=codes[:].bitcast(FP8X4), scales=scales[:], in_=grouped[:].rearrange("p c t -> p (c t)")
             )
-            bank = psum.tile([P, J], F32, name="bank")
             for u in range(N // P):
+                bank = psum.tile([P, J], F32, name="bank")
                 nc.tensor.matmul_mx(
-                    out=bank[:, u * half : (u + 1) * half],
+                    out=bank[:, 0:half],
                     lhsT=vs_picked[0][:, u * P : (u + 1) * P].bitcast(FP8X4),
                     lhsT_scale=vs_picked[1][:, u * P : (u + 1) * P],
                     rhs=codes[:].bitcast(FP8X4), rhs_scale=scales[:], start=True, stop=True,
                 )
-            result = sb_tile(f"result{h}", [P, N // P, half], F32)
-            nc.scalar.copy(result[:].rearrange("p u c -> p (u c)"), bank[:, 0 : N // P * half])
-            nc.sync.dma_start(out_view[:, :, cols], result[:])
+                result = sb_tile(f"result{h}{u}", [P, half], F32)
+                evacuate = nc.vector.tensor_copy if (h, u) == (1, 1) else nc.scalar.copy
+                evacuate(result[:], bank[:, 0:half])
+                queue = nc.scalar if (h, u) == (1, 0) else nc.sync
+                queue.dma_start(out[u * P : (u + 1) * P, cols], result[:])

@@ -71,14 +71,14 @@ def tile_picked_tokens_plain_two_filledpage_store_plain_kernel(
 
         def load_gain(name, src):
             tile = sb_tile(name, [P, PACK], F32)
-            nc.sync.dma_start(tile[:], src.rearrange("(p t) o -> p (t o)", t=PACK))
+            nc.gpsimd.dma_start(tile[:], src.rearrange("(p t) o -> p (t o)", t=PACK))
             return tile
 
-        xt_plane = zero(nc.vector, sb_tile("xt_plane", [P, T], U8))
-        w_folded = zero(nc.gpsimd, placed("w_folded", [P, 2 * R], U8, 512))
+        xt_plane = zero(nc.gpsimd, sb_tile("xt_plane", [P, T], U8))
+        w_folded = zero(nc.vector, placed("w_folded", [P, 2 * R], U8, 512))
         xo_plane = zero(nc.vector, placed("xo_plane", [P, T], U8, 11776))
-        w2_plane = zero(nc.vector, sb_tile("w2_plane", [P, R], U8))
-        vs_plane = zero(nc.vector, sb_tile("vs_plane", [P, S], U8))
+        w2_plane = zero(nc.vector, placed("w2_plane", [P, R], U8, 14848))
+        vs_plane = zero(nc.vector, placed("vs_plane", [P, S], U8, 12800))
 
         pages = [sb_tile(f"page{t}", [P, C], F32) for t in range(PACK)]
         for page in pages:
@@ -87,20 +87,20 @@ def tile_picked_tokens_plain_two_filledpage_store_plain_kernel(
         load_plane(nc.scalar, xt_plane, xt_scales)
         l1 = load_list("l1", offs)
         xt_sb = load_fp4("xt_sb", xt_words, 5632)
-        w_sb = load_fp8(nc.gpsimd, "w_sb", w_words)
         load_folded_plane((nc.sync, nc.sync), w_folded, w_scales)
-        load_plane(nc.gpsimd, w2_plane, w2_scales)
-        l3 = load_list("l3", offs3)
+        w_sb = load_fp8(nc.gpsimd, "w_sb", w_words)
         sa_sb = load_gain("sa_sb", sa)
         w2_sb = load_fp8(nc.sync, "w2_sb", w2_words)
+        l3 = load_list("l3", offs3)
         l4 = load_list("l4", offs4)
         l2 = load_list("l2", offs2)
         xo_sb = load_fp4("xo_sb", xo_words, 9728)
         load_plane(nc.sync, xo_plane, xo_scales)
+        load_plane(nc.sync, w2_plane, w2_scales)
         l6 = load_list("l6", offs6)
         vs_sb = load_fp8(nc.sync, "vs_sb", vs_words)
-        load_plane(nc.sync, vs_plane, vs_scales)
         l5 = load_list("l5", offs5)
+        load_plane(nc.gpsimd, vs_plane, vs_scales)
         sb_sb = load_gain("sb_sb", sb)
 
         def deal(copy, dst, src):
@@ -115,15 +115,16 @@ def tile_picked_tokens_plain_two_filledpage_store_plain_kernel(
             nc.vector.tensor_copy(dst[:], window[:].indirect(offsets))
             return dst
 
-        def product(t, dealt, picked):
-            width = picked[1].shape[1]
-            bank = psum.tile([P, J], F32, name="bank")
+        def new_bank():
+            return psum.tile([P, J], F32, name="bank")
+
+        def product(dst, t, dealt, picked):
             cols = slice(t * P, (t + 1) * P)
             nc.tensor.matmul_mx(
-                out=bank[:, 0:width], lhsT=dealt[0][:, cols].bitcast(FP8X4), lhsT_scale=dealt[1][:, cols],
+                out=dst, lhsT=dealt[0][:, cols].bitcast(FP8X4), lhsT_scale=dealt[1][:, cols],
                 rhs=picked[0].bitcast(FP4X4), rhs_scale=picked[1], start=True, stop=True,
             )
-            return bank[:, 0:width]
+            return dst
 
         a_rows = [sb_tile(f"a{t}", [P, J], F32) for t in range(PACK)]
         b_rows = [sb_tile(f"b{t}", [P, J], F32) for t in range(PACK)]
@@ -139,7 +140,8 @@ def tile_picked_tokens_plain_two_filledpage_store_plain_kernel(
         lo_plane = gather(sb_tile("xt_lo_plane", [P, hj], U8), xt_plane, l1[:, 0 : hj // 16])
         w_dealt = (w_words_dealt, deal_plane(placed("wd_plane", [P, R], U8, 2048), w_folded))
         for t in range(PACK):
-            nc.scalar.copy(a_rows[t][:, 0:hj], product(t, w_dealt, (lo_words[:], lo_plane[:])))
+            evacuate = nc.scalar.copy if t < PACK - 1 else nc.vector.tensor_copy
+            evacuate(a_rows[t][:, 0:hj], product(new_bank()[:, 0:hj], t, w_dealt, (lo_words[:], lo_plane[:])))
         hi_words = gather(
             placed("xt_hi_words", [P, hj], U16, 512), xt_sb, l1[:, hj // 16 : J // 16]
         )
@@ -148,7 +150,7 @@ def tile_picked_tokens_plain_two_filledpage_store_plain_kernel(
         )
         for t in range(PACK):
             evacuate = nc.scalar.copy if t == 0 else nc.vector.tensor_copy
-            evacuate(a_rows[t][:, hj:J], product(t, w_dealt, (hi_words[:], hi_plane[:])))
+            evacuate(a_rows[t][:, hj:J], product(new_bank()[:, 0:hj], t, w_dealt, (hi_words[:], hi_plane[:])))
 
         w2_words_dealt = placed("w2d_words", [P, R], U32, 5632)
         deal(nc.vector.tensor_copy, w2_words_dealt[:], w2_sb[:])
@@ -173,16 +175,16 @@ def tile_picked_tokens_plain_two_filledpage_store_plain_kernel(
         w2_plane_dealt = placed("w2d_plane", [P, R], U8, 11776)
         deal(nc.vector.tensor_copy, w2_plane_dealt[:], w2_plane[:])
         w2_dealt = (w2_words_dealt, w2_plane_dealt)
-        vs_words_picked = gather(placed("vsp_words", [P, N], U32, 9728), vs_sb, l6[:])
+        vs_words_picked = gather(placed("vsp_words", [P, N], U32, 14848), vs_sb, l6[:])
         for t in range(PACK):
-            nc.vector.tensor_copy(b_rows[t][:], product(t, w2_dealt, xo_picked))
+            nc.vector.tensor_copy(b_rows[t][:], product(new_bank()[:], t, w2_dealt, xo_picked))
         vs_picked = (vs_words_picked, gather(placed("vsp_plane", [P, N], U8, 11776), vs_plane, l6[:]))
-        fetched_all = placed("fetched", [P, 2, PACK, C // 2], F32, 5632)
+        fetched_all = [placed(f"fetched{h}", [P, PACK, C // 2], F32, offset) for h, offset in enumerate((5632, 12800))]
 
         half = C // 2
         for h in range(2):
             cols = slice(h * half, (h + 1) * half)
-            fetched = fetched_all[:, h]
+            fetched = fetched_all[h]
             hid = sb_tile(f"hid{h}", [P, PACK, half], BF16)
             for t in range(PACK):
                 nc.scalar.activation(
@@ -191,7 +193,9 @@ def tile_picked_tokens_plain_two_filledpage_store_plain_kernel(
                 )
                 nc.vector.tensor_tensor(hid[:, t, :], pages[t][:, cols], fetched[:, t, :], MAX)
             grouped = sb_tile(f"grouped{h}", [P, half, PACK], BF16)
-            nc.vector.tensor_copy(grouped[:], hid[:].rearrange("p t c -> p c t"))
+            nc.vector.tensor_copy(
+                grouped[:].rearrange("p (g i) t -> p g t i", i=4), hid[:].rearrange("p t (g i) -> p g t i", i=4)
+            )
             codes = sb_tile(f"codes{h}", [P, half], U32)
             scales = sb_tile(f"scales{h}", [P, half], U8)
             nc.vector.quantize_mx(

@@ -185,17 +185,18 @@ def tile_picked_tokens_plain_two_filledpage_store_plain_kernel(
         for h in range(2):
             cols = slice(h * half, (h + 1) * half)
             fetched = fetched_all[h]
-            hid = sb_tile(f"hid{h}", [P, PACK, half], BF16)
+            hid = sb_tile(f"hid{h}", [P, PACK - 1, half], BF16)
+            grouped = sb_tile(f"grouped{h}", [P, half, PACK], BF16)
             for t in range(PACK):
                 nc.scalar.activation(
                     fetched[:, t, :], b_rows[t][:].indirect(l5[:, h * half // 16 : (h + 1) * half // 16]), COPY,
                     scale=sb_sb[:, t : t + 1],
                 )
-                nc.vector.tensor_tensor(hid[:, t, :], pages[t][:, cols], fetched[:, t, :], MAX)
-            grouped = sb_tile(f"grouped{h}", [P, half, PACK], BF16)
-            nc.vector.tensor_copy(
-                grouped[:].rearrange("p (g i) t -> p g t i", i=4), hid[:].rearrange("p t (g i) -> p g t i", i=4)
-            )
+                if t < PACK - 1:
+                    nc.vector.tensor_tensor(hid[:, t, :], pages[t][:, cols], fetched[:, t, :], MAX)
+                else:
+                    nc.vector.tensor_copy(grouped[:, :, 0:t], hid[:].rearrange("p t c -> p c t"))
+                    nc.vector.tensor_tensor(grouped[:, :, t], pages[t][:, cols], fetched[:, t, :], MAX)
             codes = sb_tile(f"codes{h}", [P, half], U32)
             scales = sb_tile(f"scales{h}", [P, half], U8)
             nc.vector.quantize_mx(

from contextlib import ExitStack

import concourse.mybir as mybir

F32 = mybir.dt.float32
BF16 = mybir.dt.bfloat16
I32 = mybir.dt.int32
U32 = mybir.dt.uint32
U16 = mybir.dt.uint16
U8 = mybir.dt.uint8
FP8X4 = mybir.dt.float8_e4m3fn_x4
FP4X4 = mybir.dt.float4_e2m1fn_x4
COPY = mybir.ActivationFunctionType.Copy
MAX = mybir.AluOpType.max

P = 128
PACK = 4
J, R, T, O, C, N, S = 512, 512, 1024, 192, 256, 256, 1024
FLOPS = 2 * 512 * R * J * 2 + 2 * R * N * C


def tile_picked_tokens_plain_two_filledpage_store_plain_kernel(
    tc, xt_words, xt_scales, w_words, w_scales, xo_words, xo_scales, w2_words, w2_scales, sa, sb,
    vs_words, vs_scales, offs, offs2, offs3, offs4, offs5, offs6, out,
):
    nc = tc.nc
    with ExitStack() as ctx:
        keep = ctx.enter_context(tc.tile_pool(name="keep", bufs=1))
        reused = ctx.enter_context(tc.tile_pool(name="reused", bufs=1))
        psum = ctx.enter_context(tc.psum_pool(name="psum", bufs=8))

        def sb_tile(name, shape, dtype):
            return keep.tile(shape, dtype, name=name, align_bytes=64)

        def placed(name, shape, dtype, offset):
            return reused.tile(shape, dtype, name=name, offset=offset, align_bytes=64)

        def clock(name, src, dtype):
            tile = sb_tile(name, [P, 1], dtype)
            nc.gpsimd.tensor_copy(tile[:], src)

        def load_list(name, src):
            tile = sb_tile(name, [P, src.shape[1]], U16)
            nc.sync.dma_start(tile[:], src)
            return tile

        def zero(engine, tile):
            engine.memset(tile[:].bitcast(I32), 0)
            return tile

        def load_plane(queue, tile, src):
            for q in range(4):
                queue.dma_start(tile[32 * q : 32 * q + 4, :].bitcast(I32), src[0, 4 * q : 4 * q + 4, :].bitcast(I32))

        def load_folded_plane(queues, tile, src):
            rows = src[0].bitcast(I32).rearrange("(a b i) n -> b i a n", a=2, b=2)
            for b in range(2):
                queues[b].dma_start(
                    tile[32 * b : 32 * b + 4, :].bitcast(I32).rearrange("i (a n) -> i a n", a=2), rows[b]
                )

        def load_fp4(name, src, offset):
            tile = placed(name, [P, T], U16, offset)
            nc.sync.dma_start(tile[:].bitcast(I32), src[0].bitcast(I32))
            return tile

        def load_fp8(queue, name, src):
            tile = sb_tile(name, [P, src.shape[2]], U32)
            queue.dma_start(tile[:].bitcast(I32), src[0].rearrange("p n t -> p (n t)").bitcast(I32))
            return tile

        def load_gain(name, src):
            tile = sb_tile(name, [P, PACK], F32)
            nc.gpsimd.dma_start(tile[:], src.rearrange("(p t) o -> p (t o)", t=PACK))
            return tile

        xt_plane = zero(nc.gpsimd, sb_tile("xt_plane", [P, T], U8))
        w_folded = zero(nc.vector, placed("w_folded", [P, 2 * R], U8, 512))
        xo_plane = zero(nc.vector, placed("xo_plane", [P, T], U8, 11776))
        w2_plane = zero(nc.vector, placed("w2_plane", [P, R], U8, 14848))
        vs_plane = zero(nc.vector, placed("vs_plane", [P, S], U8, 12800))

        pages = [sb_tile(f"page{t}", [P, C], F32) for t in range(PACK)]
        for page in pages:
            nc.vector.memset(page[:], 0.0)

        load_plane(nc.scalar, xt_plane, xt_scales)
        l1 = load_list("l1", offs)
        xt_sb = load_fp4("xt_sb", xt_words, 5632)
        load_folded_plane((nc.sync, nc.sync), w_folded, w_scales)
        w_sb = load_fp8(nc.gpsimd, "w_sb", w_words)
        sa_sb = load_gain("sa_sb", sa)
        w2_sb = load_fp8(nc.sync, "w2_sb", w2_words)
        l3 = load_list("l3", offs3)
        l4 = load_list("l4", offs4)
        l2 = load_list("l2", offs2)
        xo_sb = load_fp4("xo_sb", xo_words, 9728)
        load_plane(nc.sync, xo_plane, xo_scales)
        load_plane(nc.sync, w2_plane, w2_scales)
        l6 = load_list("l6", offs6)
        vs_sb = load_fp8(nc.sync, "vs_sb", vs_words)
        l5 = load_list("l5", offs5)
        load_plane(nc.gpsimd, vs_plane, vs_scales)
        sb_sb = load_gain("sb_sb", sb)

        def deal(copy, dst, src):
            copy(dst.rearrange("p (t m) -> p m t", t=PACK), src.rearrange("p (m t) -> p m t", t=PACK))

        def deal_plane(dealt, folded):
            nc.vector.tensor_copy(folded[64:128, 0:R].bitcast(I32), folded[0:64, R : 2 * R].bitcast(I32))
            deal(nc.vector.tensor_copy, dealt[:], folded[:, 0:R])
            return dealt

        def gather(dst, window, offsets):
            nc.vector.tensor_copy(dst[:], window[:].indirect(offsets))
            return dst

        def new_bank():
            return psum.tile([P, J], F32, name="bank")

        def product(dst, t, dealt, picked):
            cols = slice(t * P, (t + 1) * P)
            nc.tensor.matmul_mx(
                out=dst, lhsT=dealt[0][:, cols].bitcast(FP8X4), lhsT_scale=dealt[1][:, cols],
                rhs=picked[0].bitcast(FP4X4), rhs_scale=picked[1], start=True, stop=True,
            )
            return dst

        a_rows = [sb_tile(f"a{t}", [P, J], F32) for t in range(PACK)]
        b_rows = [sb_tile(f"b{t}", [P, J], F32) for t in range(PACK)]
        hj = J // 2

        w_words_dealt = placed("wd_words", [P, R], U32, 3072)
        for t in (0, 2):
            nc.scalar.copy(
                w_words_dealt[:].rearrange("p (t m) -> p m t", t=PACK)[:, :, t : t + 2],
                w_sb[:].rearrange("p (m t) -> p m t", t=PACK)[:, :, t : t + 2],
            )
        lo_words = gather(sb_tile("xt_lo_words", [P, hj], U16), xt_sb, l1[:, 0 : hj // 16])
        lo_plane = gather(sb_tile("xt_lo_plane", [P, hj], U8), xt_plane, l1[:, 0 : hj // 16])
        w_dealt = (w_words_dealt, deal_plane(placed("wd_plane", [P, R], U8, 2048), w_folded))
        for t in range(PACK):
            evacuate = nc.scalar.copy if t < PACK - 1 else nc.vector.tensor_copy
            evacuate(a_rows[t][:, 0:hj], product(new_bank()[:, 0:hj], t, w_dealt, (lo_words[:], lo_plane[:])))
        hi_words = gather(
            placed("xt_hi_words", [P, hj], U16, 512), xt_sb, l1[:, hj // 16 : J // 16]
        )
        hi_plane = gather(
            placed("xt_hi_plane", [P, hj], U8, 1024), xt_plane, l1[:, hj // 16 : J // 16]
        )
        for t in range(PACK):
            evacuate = nc.scalar.copy if t == 0 else nc.vector.tensor_copy
            evacuate(a_rows[t][:, hj:J], product(new_bank()[:, 0:hj], t, w_dealt, (hi_words[:], hi_plane[:])))

        w2_words_dealt = placed("w2d_words", [P, R], U32, 5632)
        deal(nc.vector.tensor_copy, w2_words_dealt[:], w2_sb[:])
        h1 = [sb_tile(f"h1_{t}", [P, O], F32) for t in range(PACK)]

        def fetch_a(t):
            nc.scalar.activation(h1[t][:], a_rows[t][:].indirect(l3[:]), COPY, scale=sa_sb[:, t : t + 1])

        def fill(t):
            nc.scalar.activation(pages[t][:].indirect(l4[:]), h1[t][:], COPY)

        for t in range(PACK):
            fetch_a(t)
        for t in range(PACK):
            fill(t)


        xo_picked = (
            gather(placed("xop_words", [P, J], U16, 3072), xo_sb, l2[:])[:],
            gather(placed("xop_plane", [P, J], U8, 4096), xo_plane, l2[:])[:],
        )
        w2_plane_dealt = placed("w2d_plane", [P, R], U8, 11776)
        deal(nc.vector.tensor_copy, w2_plane_dealt[:], w2_plane[:])
        w2_dealt = (w2_words_dealt, w2_plane_dealt)
        vs_words_picked = gather(placed("vsp_words", [P, N], U32, 14848), vs_sb, l6[:])
        for t in range(PACK):
            nc.vector.tensor_copy(b_rows[t][:], product(new_bank()[:], t, w2_dealt, xo_picked))
        vs_picked = (vs_words_picked, gather(placed("vsp_plane", [P, N], U8, 11776), vs_plane, l6[:]))
        fetched_all = [placed(f"fetched{h}", [P, PACK, C // 2], F32, offset) for h, offset in enumerate((5632, 12800))]

        half = C // 2
        for h in range(2):
            cols = slice(h * half, (h + 1) * half)
            fetched = fetched_all[h]
            hid = sb_tile(f"hid{h}", [P, PACK - 1, half], BF16)
            grouped = sb_tile(f"grouped{h}", [P, half, PACK], BF16)
            for t in range(PACK):
                nc.scalar.activation(
                    fetched[:, t, :], b_rows[t][:].indirect(l5[:, h * half // 16 : (h + 1) * half // 16]), COPY,
                    scale=sb_sb[:, t : t + 1],
                )
                if t < PACK - 1:
                    nc.vector.tensor_tensor(hid[:, t, :], pages[t][:, cols], fetched[:, t, :], MAX)
                else:
                    nc.vector.tensor_copy(grouped[:, :, 0:t], hid[:].rearrange("p t c -> p c t"))
                    nc.vector.tensor_tensor(grouped[:, :, t], pages[t][:, cols], fetched[:, t, :], MAX)
            codes = sb_tile(f"codes{h}", [P, half], U32)
            scales = sb_tile(f"scales{h}", [P, half], U8)
            nc.vector.quantize_mx(
                out=codes[:].bitcast(FP8X4), scales=scales[:], in_=grouped[:].rearrange("p c t -> p (c t)")
            )
            for u in range(N // P):
                bank = psum.tile([P, J], F32, name="bank")
                nc.tensor.matmul_mx(
                    out=bank[:, 0:half],
                    lhsT=vs_picked[0][:, u * P : (u + 1) * P].bitcast(FP8X4),
                    lhsT_scale=vs_picked[1][:, u * P : (u + 1) * P],
                    rhs=codes[:].bitcast(FP8X4), rhs_scale=scales[:], start=True, stop=True,
                )
                result = sb_tile(f"result{h}{u}", [P, half], F32)
                evacuate = nc.vector.tensor_copy if (h, u) == (1, 1) else nc.scalar.copy
                evacuate(result[:], bank[:, 0:half])
                queue = nc.scalar if (h, u) == (1, 0) else nc.sync
                queue.dma_start(out[u * P : (u + 1) * P, cols], result[:])
